import numpy as np
import ml_dtypes


def mxq(x, axis, fmt="e4m3"):
    dtype, down = {"e4m3": (ml_dtypes.float8_e4m3fn, 7), "e5m2": (ml_dtypes.float8_e5m2, 14)}[fmt]
    v = np.moveaxis(np.asarray(x, np.float32).astype(ml_dtypes.bfloat16).astype(np.float64), axis, -1)
    blocks = v.reshape(v.shape[:-1] + (-1, 32))
    amax = np.abs(blocks).max(-1, keepdims=True)
    byte = np.maximum(np.where(amax > 0, np.frexp(amax)[1] - 1 + 127, 0) - down, 1)
    scale = np.exp2(byte - 127.0)
    codes = (blocks / scale).astype(np.float32).astype(dtype).astype(np.float64)
    return np.moveaxis((codes * scale).reshape(v.shape), -1, axis)


WIDE = False


def mx_kscale(k):
    if not WIDE:
        return np.ones(k)
    levels = np.array([10, -10, 5, -5, 0])
    if k % 512:
        return np.exp2(np.random.permutation(np.resize(levels, k // 32))).repeat(32)
    a = np.empty((k // 512, 16))
    for p in range(k // 512):
        a[p, :8] = np.random.permutation(np.resize(levels, 8))
        for g in range(8):
            far = levels[np.abs(levels - a[p, g]) >= 10]
            a[p, g + 8] = far[np.random.randint(len(far))]
    return np.exp2(a.ravel()).repeat(32)


def f64(x):
    return np.asarray(x).astype(np.float64)


def striped(idx):
    return np.tile(idx.reshape(-1, 16).T, (8, 1)).astype(np.uint16)


def unstriped(offs):
    return offs[:16].T.reshape(-1).astype(np.int64)


def striped8(idx):
    return np.concatenate([x.reshape(-1, 16).T for x in idx]).astype(np.uint16)


def runs(offs, k):
    lists = np.stack([offs[16 * r : 16 * r + 16].T.reshape(-1) for r in range(8)]).astype(np.int64)
    return lists[np.arange(k) % 512 // 64]


def pack_weight(w):
    k, n = w.shape
    w = f64(np.asarray(w, np.float32).astype(ml_dtypes.bfloat16)).reshape(k // 32, 32, n)
    amax = np.abs(w).max(1)
    byte = np.clip(np.where(amax > 0, np.frexp(amax)[1] - 1 + 127 - 7, 1), 1, 254)
    scaled = (w * np.exp2(127.0 - byte)[:, None, :]).reshape(k, n).astype(np.float32)
    words = np.ascontiguousarray(scaled.reshape(k // 512, 128, 4, n).transpose(0, 1, 3, 2)).astype(ml_dtypes.float8_e4m3fn).view(np.uint8)
    return words, np.ascontiguousarray(byte.astype(np.uint8).reshape(k // 512, 16, n))


def unpack_weight(words, scales):
    g, p, n, _ = words.shape
    vals = np.ascontiguousarray(words).view(ml_dtypes.float8_e4m3fn).astype(np.float64) * np.repeat(np.exp2(scales.astype(np.float64) - 127.0), 8, axis=1)[..., None]
    return vals.transpose(0, 1, 3, 2).reshape(g * 512, n)


K, T, S, N, H, C = 512, 2048, 512, 512, 512, 512


def setup_inputs():
    n = np.random.standard_normal
    s = mx_kscale(K)[:, None]
    u = mx_kscale(S)
    packed_xT = pack_weight(n((K, T)) * s)
    return {
        "x_words": packed_xT[0],
        "x_scales": packed_xT[1],
        "w1": (n((K, H)) / np.sqrt(K) / s).astype(np.float32),
        "gn": (np.random.uniform(0.5, 1.5, (H, 1)) * u[:, None]).astype(np.float32),
        "w2": (n((H, N)) / np.sqrt(H) / u[:, None]).astype(np.float32),
        "gs": (np.random.uniform(0.5, 1.5, (K, 1)) / s).astype(np.float32),
        "offs": striped(np.random.permutation(T)[:S]),
        "n1": striped8(np.stack([np.random.permutation(S) for _ in range(8)])),
        "n2": striped8(np.stack([np.random.permutation(S) for _ in range(8)])),
        "n3": striped8(np.stack([np.random.permutation(S) for _ in range(8)])),
        "n4": striped8(np.stack([np.random.permutation(S) for _ in range(8)])),
        "cand": striped(np.random.permutation(T)[:C]),
        "n5": striped(np.random.permutation(S)),
        "n6": striped(np.random.permutation(S)),
    }


def reference(x_words, x_scales, w1, gn, w2, gs, offs, n1, n2, n3, n4, cand, n5, n6):
    xq = unpack_weight(x_words, x_scales)[:, unstriped(offs)]
    y = mxq(f64(w1), 0, "e4m3").T @ xq
    st = np.maximum(y, y[np.arange(H)[:, None], runs(n1, H)])
    z = f64(gn) * (st[np.arange(H)[:, None], runs(n2, H)] - (0.5 * y))
    a = mxq(f64(w2), 0, "e4m3").T @ mxq(z, 0, "e4m3")
    x_cand = unpack_weight(x_words, x_scales)[:, unstriped(cand)]
    st2 = y - (y[np.arange(H)[:, None], runs(n3, H)])
    z2 = f64(gs) * (np.maximum(st2, st2[np.arange(H)[:, None], runs(n4, H)]))
    b = 0.0625 * ((x_cand.T @ mxq(z2, 0, "e4m3")))
    return np.maximum(a, b[:, unstriped(n6)]) - (np.minimum(a[:, unstriped(n5)], b))

@@ -1,0 +1,195 @@
+from contextlib import ExitStack
+
+import concourse.mybir as mybir
+
+K, T, S = 512, 2048, 512
+P = 128
+PACK = 4
+FLOPS = 3 * 2 * 512 * 512 * 512
+
+F32 = mybir.dt.float32
+BF16 = mybir.dt.bfloat16
+I32 = mybir.dt.int32
+U32 = mybir.dt.uint32
+U16 = mybir.dt.uint16
+U8 = mybir.dt.uint8
+FP8X4 = mybir.dt.float8_e4m3fn_x4
+ALU = mybir.AluOpType
+COPY = mybir.ActivationFunctionType.Copy
+
+
+def tile_picked_fkcdmaxbhopbhopmx_none_p_kernel(
+    tc, x_words, x_scales, w1, gn, w2, gs, offs, n1, n2, n3, n4, cand, n5, n6, out
+):
+    nc = tc.nc
+    with ExitStack() as ctx:
+        keep = ctx.enter_context(tc.tile_pool(name="keep", bufs=1))
+        psum = ctx.enter_context(tc.psum_pool(name="psum", bufs=1))
+
+        def load_list(name, src):
+            t = keep.tile([P, S // 16], U16, name=name)
+            nc.sync.dma_start(t[:], src)
+            return t
+
+        def gather(engine, dst, window, offsets):
+            if engine == "vector":
+                nc.vector.tensor_copy(dst, window[:].indirect(offsets[:]))
+            else:
+                nc.scalar.activation(dst, window[:].indirect(offsets[:]), COPY)
+
+        def mx(acc, lw, ls, m, rw, rs):
+            cols = slice(P * m, P * (m + 1))
+            nc.tensor.matmul_mx(
+                out=acc[:],
+                lhsT=lw[:, cols].bitcast(FP8X4),
+                lhsT_scale=ls[:, cols],
+                rhs=rw[:].bitcast(FP8X4),
+                rhs_scale=rs[:],
+                start=True,
+                stop=True,
+            )
+
+        offs_t = load_list("offs_t", offs)
+        cand_t = load_list("cand_t", cand)
+        xs = keep.tile([P, T], U8, name="xs", align_bytes=64)
+        nc.vector.memset(xs[:].bitcast(I32), 0)
+        for q in range(4):
+            nc.scalar.dma_start(xs[32 * q : 32 * q + 4, :].bitcast(I32), x_scales[0, 4 * q : 4 * q + 4, :].bitcast(I32))
+        w1_raw = keep.tile([P, PACK, 512], F32, name="w1_raw")
+        nc.sync.dma_start(w1_raw[:], w1.rearrange("(p j) c -> p j c", j=PACK))
+        xw = keep.tile([P, T], I32, name="xw", align_bytes=64)
+        nc.sync.dma_start(xw[:], x_words[0].rearrange("p n t -> p (n t)").bitcast(I32))
+        n1_t = load_list("n1_t", n1)
+        n3_t = load_list("n3_t", n3)
+        w2_raw = keep.tile([P, PACK, 512], F32, name="w2_raw")
+        nc.sync.dma_start(w2_raw[:], w2.rearrange("(p j) c -> p j c", j=PACK))
+        n2_t = load_list("n2_t", n2)
+        n4_t = load_list("n4_t", n4)
+        gn_t = keep.tile([P, PACK], F32, name="gn_t")
+        nc.sync.dma_start(gn_t[:], gn.rearrange("(p t) o -> p (t o)", t=PACK))
+        gs_t = keep.tile([P, PACK], F32, name="gs_t")
+        nc.sync.dma_start(gs_t[:], gs.rearrange("(p t) o -> p (t o)", t=PACK))
+        n5_t = load_list("n5_t", n5)
+        n6_t = load_list("n6_t", n6)
+
+        y_win = [keep.tile([P, 2 * S], F32, name="y_win%d" % t) for t in range(4)]
+        st_win = [keep.tile([P, 2 * S], F32, name="st_win%d" % t) for t in range(4)]
+        s2_win = [keep.tile([P, 2 * S], F32, name="s2_win%d" % t) for t in range(4)]
+        for t in range(4):
+            nc.vector.memset(y_win[t][:, S:], 0.0)
+
+        def scale_quantise(name, planes, gain):
+            grouped = keep.tile([P, 4 * S], BF16, name=name + "_g", align_bytes=64)
+            words = keep.tile([P, S], U32, name=name + "_w", align_bytes=64)
+            scales = keep.tile([P, S], U8, name=name + "_s", align_bytes=64)
+            gv = grouped[:].rearrange("p (c i t) -> p c t i", i=4, t=4)
+            pv = planes[:].rearrange("p t (c i) -> p c t i", i=4)
+            gb = gain[:].unsqueeze(1).unsqueeze(3).to_broadcast([P, 64, 4, 4])
+            for h in range(2):
+                nc.vector.tensor_tensor(gv[:, 64 * h : 64 * (h + 1)], pv[:, 64 * h : 64 * (h + 1)], gb, ALU.mult)
+            for h in range(2):
+                cols = slice(256 * h, 256 * (h + 1))
+                nc.vector.quantize_mx(
+                    out=words[:, cols].bitcast(FP8X4), scales=scales[:, cols], in_=grouped[:, 1024 * h : 1024 * (h + 1)]
+                )
+            return words, scales
+
+        pick_w = keep.tile([P, S], U32, name="pick_w", align_bytes=64)
+        pick_s = keep.tile([P, S], U8, name="pick_s", align_bytes=64)
+        cand_w = keep.tile([P, S], U32, name="cand_w", align_bytes=64)
+        cand_s = keep.tile([P, S], U8, name="cand_s", align_bytes=64)
+        nc.vector.tensor_copy(pick_s[:], xs[:].indirect(offs_t[:]))
+
+        w1_g = keep.tile([P, 4 * 512], BF16, name="w1_g", align_bytes=64)
+        w1_v = w1_g[:].rearrange("p (t m j) -> p m j t", t=4, j=4)
+        w1_r = w1_raw[:].rearrange("p j (m t) -> p m j t", t=4)
+        nc.scalar.copy(w1_v[:, :64], w1_r[:, :64])
+        nc.vector.tensor_copy(w1_v[:, 64:], w1_r[:, 64:])
+        nc.vector.tensor_copy(cand_s[:], xs[:].indirect(cand_t[:]))
+        w1_w = keep.tile([P, 512], U32, name="w1_w", align_bytes=64)
+        w1_s = keep.tile([P, 512], U8, name="w1_s", align_bytes=64)
+        nc.vector.quantize_mx(out=w1_w[:].bitcast(FP8X4), scales=w1_s[:], in_=w1_g[:])
+        nc.vector.tensor_copy(pick_w[:], xw[:].bitcast(U32).indirect(offs_t[:]))
+        y_ps = []
+        for t in range(4):
+            acc = psum.tile([P, S], F32, name="y_ps%d" % t, tag="yb%d" % t)
+            mx(acc, w1_w, w1_s, t, pick_w, pick_s)
+            y_ps.append(acc)
+        nc.vector.tensor_copy(cand_w[:], xw[:].bitcast(U32).indirect(cand_t[:]))
+
+        w2_g = keep.tile([P, 4 * 512], BF16, name="w2_g", align_bytes=64)
+        nc.gpsimd.tensor_scalar(
+            w2_g[:].rearrange("p (c j) -> p c j", j=4),
+            w2_raw[:].rearrange("p j c -> p c j"),
+            1.0,
+            0.0,
+            ALU.mult,
+            ALU.add,
+        )
+        w2_w = keep.tile([P, 512], U32, name="w2_w", align_bytes=64)
+        w2_s = keep.tile([P, 512], U8, name="w2_s", align_bytes=64)
+
+        for t in range(4):
+            nc.scalar.copy(y_win[t][:, :S], y_ps[t][:])
+        g2 = [keep.tile([P, S], F32, name="g2_%d" % t) for t in range(4)]
+        z_pl = keep.tile([P, 4, S], F32, name="z_pl")
+
+        def z_plane(t):
+            nc.vector.scalar_tensor_tensor(z_pl[:, t, :], y_ps[t][:], -0.5, g2[t][:], ALU.mult, ALU.add)
+
+        for t in range(4):
+            gather("vector", st_win[t][:, S:], y_win[t], n1_t)
+            gather("scalar", s2_win[t][:, S:], y_win[t], n3_t)
+            nc.gpsimd.tensor_tensor(s2_win[t][:, :S], y_win[t][:, :S], s2_win[t][:, S:], ALU.subtract)
+            if t > 0:
+                nc.vector.tensor_tensor(st_win[t - 1][:, :S], y_ps[t - 1][:], st_win[t - 1][:, S:], ALU.max)
+                gather("scalar", g2[t - 1][:], st_win[t - 1], n2_t)
+        nc.vector.quantize_mx(out=w2_w[:].bitcast(FP8X4), scales=w2_s[:], in_=w2_g[:])
+        nc.vector.tensor_tensor(st_win[3][:, :S], y_ps[3][:], st_win[3][:, S:], ALU.max)
+        z_plane(0)
+        gather("vector", g2[3][:], st_win[3], n2_t)
+        for t in range(1, 4):
+            z_plane(t)
+
+        g4 = [keep.tile([P, S], F32, name="g4_%d" % t) for t in range(4)]
+        for t in range(4):
+            gather("scalar", g4[t][:], s2_win[t], n4_t)
+        z_w, z_s = scale_quantise("z", z_pl, gn_t)
+        a_ps = []
+        for m in range(4):
+            acc = psum.tile([P, S], F32, name="a_ps%d" % m, tag="ab%d" % m)
+            mx(acc, w2_w, w2_s, m, z_w, z_s)
+            a_ps.append(acc)
+
+        z2_pl = keep.tile([P, 4, S], F32, name="z2_pl")
+        for t in range(4):
+            nc.vector.tensor_tensor(z2_pl[:, t, :], s2_win[t][:, :S], g4[t][:], ALU.max)
+        z2_w, z2_s = scale_quantise("z2", z2_pl, gs_t)
+
+        g5 = g2
+        for m in range(4):
+            nc.scalar.copy(st_win[m][:, :S], a_ps[m][:])
+            gather("scalar", g5[m][:], st_win[m], n5_t)
+
+        b_ps = []
+        for m in range(4):
+            acc = psum.tile([P, S], F32, name="b_ps%d" % m, tag="yb%d" % m)
+            mx(acc, cand_w, cand_s, m, z2_w, z2_s)
+            b_ps.append(acc)
+        g6 = g4
+        for m in range(2):
+            nc.vector.tensor_scalar(s2_win[m][:, :S], b_ps[m][:], 0.0625, None, ALU.mult)
+        gather("vector", g6[0][:], s2_win[0], n6_t)
+        for m in range(1, 4):
+            if m >= 2:
+                nc.scalar.activation(s2_win[m][:, :S], b_ps[m][:], COPY, scale=0.0625)
+            gather("scalar", g6[m][:], s2_win[m], n6_t)
+        for m in range(4):
+            lo = keep.tile([P, S], F32, name="lo%d" % m)
+            nc.vector.scalar_tensor_tensor(lo[:], b_ps[m][:], 0.0625, g5[m][:], ALU.mult, ALU.min)
+            hi = keep.tile([P, S], F32, name="hi%d" % m)
+            nc.vector.tensor_tensor(hi[:], a_ps[m][:], g6[m][:], ALU.max)
+            res = keep.tile([P, S], F32, name="res%d" % m)
+            eng = nc.vector if m == 3 else nc.gpsimd
+            eng.tensor_tensor(res[:], hi[:], lo[:], ALU.subtract)
+            nc.sync.dma_start(out[P * m : P * (m + 1), :], res[:])

@@ -24,6 +24,7 @@ def tile_picked_fkcdmaxbhopbhopmx_none_p_kernel(
     nc = tc.nc
     with ExitStack() as ctx:
         keep = ctx.enter_context(tc.tile_pool(name="keep", bufs=1))
+        reuse = ctx.enter_context(tc.tile_pool(name="reuse", bufs=1))
         psum = ctx.enter_context(tc.psum_pool(name="psum", bufs=1))
 
         def load_list(name, src):
@@ -37,34 +38,37 @@ def tile_picked_fkcdmaxbhopbhopmx_none_p_kernel(
             else:
                 nc.scalar.activation(dst, window[:].indirect(offsets[:]), COPY)
 
-        def mx(acc, lw, ls, m, rw, rs):
+        def mx(acc, lw, ls, m, rw, rs, c0=0, c1=S):
             cols = slice(P * m, P * (m + 1))
             nc.tensor.matmul_mx(
-                out=acc[:],
+                out=acc[:, c0:c1],
                 lhsT=lw[:, cols].bitcast(FP8X4),
                 lhsT_scale=ls[:, cols],
-                rhs=rw[:].bitcast(FP8X4),
-                rhs_scale=rs[:],
+                rhs=rw[:, c0:c1].bitcast(FP8X4),
+                rhs_scale=rs[:, c0:c1],
                 start=True,
                 stop=True,
             )
 
-        offs_t = load_list("offs_t", offs)
-        cand_t = load_list("cand_t", cand)
         xs = keep.tile([P, T], U8, name="xs", align_bytes=64)
         nc.vector.memset(xs[:].bitcast(I32), 0)
         for q in range(4):
             nc.scalar.dma_start(xs[32 * q : 32 * q + 4, :].bitcast(I32), x_scales[0, 4 * q : 4 * q + 4, :].bitcast(I32))
-        w1_raw = keep.tile([P, PACK, 512], F32, name="w1_raw")
-        nc.sync.dma_start(w1_raw[:], w1.rearrange("(p j) c -> p j c", j=PACK))
-        xw = keep.tile([P, T], I32, name="xw", align_bytes=64)
-        nc.sync.dma_start(xw[:], x_words[0].rearrange("p n t -> p (n t)").bitcast(I32))
+        offs_t = load_list("offs_t", offs)
+        cand_t = load_list("cand_t", cand)
         n1_t = load_list("n1_t", n1)
         n3_t = load_list("n3_t", n3)
-        w2_raw = keep.tile([P, PACK, 512], F32, name="w2_raw")
-        nc.sync.dma_start(w2_raw[:], w2.rearrange("(p j) c -> p j c", j=PACK))
+        xw = keep.tile([P, T], I32, name="xw", align_bytes=64)
+        nc.sync.dma_start(xw[:], x_words[0].rearrange("p n t -> p (n t)").bitcast(I32))
+        w1_raw = []
+        for h in range(2):
+            r = keep.tile([P, PACK, 256], F32, name="w1_raw%d" % h)
+            nc.sync.dma_start(r[:], w1.rearrange("(p j) c -> p j c", j=PACK)[:, :, 256 * h : 256 * (h + 1)])
+            w1_raw.append(r)
         n2_t = load_list("n2_t", n2)
         n4_t = load_list("n4_t", n4)
+        w2_raw = keep.tile([P, PACK, 512], F32, name="w2_raw")
+        nc.sync.dma_start(w2_raw[:], w2.rearrange("(p j) c -> p j c", j=PACK))
         gn_t = keep.tile([P, PACK], F32, name="gn_t")
         nc.sync.dma_start(gn_t[:], gn.rearrange("(p t) o -> p (t o)", t=PACK))
         gs_t = keep.tile([P, PACK], F32, name="gs_t")
@@ -96,26 +100,28 @@ def tile_picked_fkcdmaxbhopbhopmx_none_p_kernel(
 
         pick_w = keep.tile([P, S], U32, name="pick_w", align_bytes=64)
         pick_s = keep.tile([P, S], U8, name="pick_s", align_bytes=64)
-        cand_w = keep.tile([P, S], U32, name="cand_w", align_bytes=64)
-        cand_s = keep.tile([P, S], U8, name="cand_s", align_bytes=64)
+        nc.vector.tensor_copy(pick_w[:], xw[:].bitcast(U32).indirect(offs_t[:]))
         nc.vector.tensor_copy(pick_s[:], xs[:].indirect(offs_t[:]))
 
-        w1_g = keep.tile([P, 4 * 512], BF16, name="w1_g", align_bytes=64)
+        w1_g = reuse.tile([P, 4 * 512], BF16, name="w1_g", offset=0, align_bytes=64)
         w1_v = w1_g[:].rearrange("p (t m j) -> p m j t", t=4, j=4)
-        w1_r = w1_raw[:].rearrange("p j (m t) -> p m j t", t=4)
-        nc.scalar.copy(w1_v[:, :64], w1_r[:, :64])
-        nc.vector.tensor_copy(w1_v[:, 64:], w1_r[:, 64:])
-        nc.vector.tensor_copy(cand_s[:], xs[:].indirect(cand_t[:]))
+        w1_r = [r[:].rearrange("p j (m t) -> p m j t", t=4) for r in w1_raw]
+        nc.scalar.copy(w1_v[:, :64], w1_r[0])
+        nc.scalar.copy(w1_v[:, 64:88], w1_r[1][:, :24])
+        nc.vector.tensor_copy(w1_v[:, 88:], w1_r[1][:, 24:])
         w1_w = keep.tile([P, 512], U32, name="w1_w", align_bytes=64)
         w1_s = keep.tile([P, 512], U8, name="w1_s", align_bytes=64)
-        nc.vector.quantize_mx(out=w1_w[:].bitcast(FP8X4), scales=w1_s[:], in_=w1_g[:])
-        nc.vector.tensor_copy(pick_w[:], xw[:].bitcast(U32).indirect(offs_t[:]))
         y_ps = []
         for t in range(4):
+            cols = slice(P * t, P * (t + 1))
+            nc.vector.quantize_mx(out=w1_w[:, cols].bitcast(FP8X4), scales=w1_s[:, cols], in_=w1_g[:, 512 * t : 512 * (t + 1)])
             acc = psum.tile([P, S], F32, name="y_ps%d" % t, tag="yb%d" % t)
             mx(acc, w1_w, w1_s, t, pick_w, pick_s)
             y_ps.append(acc)
+        cand_w = reuse.tile([P, S], U32, name="cand_w", offset=0, align_bytes=64)
+        cand_s = reuse.tile([P, S], U8, name="cand_s", offset=2048, align_bytes=64)
         nc.vector.tensor_copy(cand_w[:], xw[:].bitcast(U32).indirect(cand_t[:]))
+        nc.vector.tensor_copy(cand_s[:], xs[:].indirect(cand_t[:]))
 
         w2_g = keep.tile([P, 4 * 512], BF16, name="w2_g", align_bytes=64)
         nc.gpsimd.tensor_scalar(
@@ -129,67 +135,88 @@ def tile_picked_fkcdmaxbhopbhopmx_none_p_kernel(
         w2_w = keep.tile([P, 512], U32, name="w2_w", align_bytes=64)
         w2_s = keep.tile([P, 512], U8, name="w2_s", align_bytes=64)
 
-        for t in range(4):
-            nc.scalar.copy(y_win[t][:, :S], y_ps[t][:])
-        g2 = [keep.tile([P, S], F32, name="g2_%d" % t) for t in range(4)]
-        z_pl = keep.tile([P, 4, S], F32, name="z_pl")
+        def evacuate(engine, dst, src, scale):
+            if engine == "vector":
+                nc.vector.tensor_scalar(dst, src, scale, None, ALU.mult)
+            else:
+                nc.scalar.activation(dst, src, COPY, scale=scale)
 
-        def z_plane(t):
-            nc.vector.scalar_tensor_tensor(z_pl[:, t, :], y_ps[t][:], -0.5, g2[t][:], ALU.mult, ALU.add)
+        for t in range(4):
+            evacuate("scalar", y_win[t][:, :S], y_ps[t][:], 1.0)
+        g2 = [keep.tile([P, S], F32, name="g2_%d" % t) for t in range(4)]
+        g4 = [keep.tile([P, S], F32, name="g4_%d" % t) for t in range(4)]
+        planes = keep.tile([P, 4, S], F32, name="planes")
 
         for t in range(4):
             gather("vector", st_win[t][:, S:], y_win[t], n1_t)
+        for t in range(4):
             gather("scalar", s2_win[t][:, S:], y_win[t], n3_t)
             nc.gpsimd.tensor_tensor(s2_win[t][:, :S], y_win[t][:, :S], s2_win[t][:, S:], ALU.subtract)
-            if t > 0:
-                nc.vector.tensor_tensor(st_win[t - 1][:, :S], y_ps[t - 1][:], st_win[t - 1][:, S:], ALU.max)
-                gather("scalar", g2[t - 1][:], st_win[t - 1], n2_t)
-        nc.vector.quantize_mx(out=w2_w[:].bitcast(FP8X4), scales=w2_s[:], in_=w2_g[:])
-        nc.vector.tensor_tensor(st_win[3][:, :S], y_ps[3][:], st_win[3][:, S:], ALU.max)
-        z_plane(0)
-        gather("vector", g2[3][:], st_win[3], n2_t)
-        for t in range(1, 4):
-            z_plane(t)
-
-        g4 = [keep.tile([P, S], F32, name="g4_%d" % t) for t in range(4)]
         for t in range(4):
-            gather("scalar", g4[t][:], s2_win[t], n4_t)
-        z_w, z_s = scale_quantise("z", z_pl, gn_t)
+            nc.vector.tensor_tensor(st_win[t][:, :S], y_ps[t][:], st_win[t][:, S:], ALU.max)
+        for t in range(4):
+            gather("scalar", g2[t][:], st_win[t], n2_t)
+        nc.vector.quantize_mx(out=w2_w[:].bitcast(FP8X4), scales=w2_s[:], in_=w2_g[:])
+        for t in range(4):
+            nc.vector.scalar_tensor_tensor(planes[:, t, :], y_ps[t][:], -0.5, g2[t][:], ALU.mult, ALU.add)
+        z_w, z_s = scale_quantise("z", planes, gn_t)
         a_ps = []
         for m in range(4):
             acc = psum.tile([P, S], F32, name="a_ps%d" % m, tag="ab%d" % m)
             mx(acc, w2_w, w2_s, m, z_w, z_s)
             a_ps.append(acc)
 
-        z2_pl = keep.tile([P, 4, S], F32, name="z2_pl")
         for t in range(4):
-            nc.vector.tensor_tensor(z2_pl[:, t, :], s2_win[t][:, :S], g4[t][:], ALU.max)
-        z2_w, z2_s = scale_quantise("z2", z2_pl, gs_t)
+            gather("scalar", g4[t][:], s2_win[t], n4_t)
+        for t in range(4):
+            nc.vector.tensor_tensor(planes[:, t, :], s2_win[t][:, :S], g4[t][:], ALU.max)
+        z2_w, z2_s = scale_quantise("z2", planes, gs_t)
 
-        g5 = g2
+        a_win, b_win = st_win, s2_win
+        g5 = [g2[0][:], g2[1][:], g2[2][:], planes[:, 3, :]]
         for m in range(4):
-            nc.scalar.copy(st_win[m][:, :S], a_ps[m][:])
-            gather("scalar", g5[m][:], st_win[m], n5_t)
+            evacuate("scalar", a_win[m][:, :S], a_ps[m][:], 1.0)
+        for m in range(4):
+            gather("vector" if m == 3 else "scalar", g5[m], a_win[m], n5_t)
 
         b_ps = []
         for m in range(4):
             acc = psum.tile([P, S], F32, name="b_ps%d" % m, tag="yb%d" % m)
-            mx(acc, cand_w, cand_s, m, z2_w, z2_s)
+            mx(acc, cand_w, cand_s, m, z2_w, z2_s, 0, S // 2)
+            mx(acc, cand_w, cand_s, m, z2_w, z2_s, S // 2, S)
             b_ps.append(acc)
         g6 = g4
-        for m in range(2):
-            nc.vector.tensor_scalar(s2_win[m][:, :S], b_ps[m][:], 0.0625, None, ALU.mult)
-        gather("vector", g6[0][:], s2_win[0], n6_t)
+        lo = [keep.tile([P, S], F32, name="lo%d" % m) for m in range(4)]
+        hi = [keep.tile([P, S], F32, name="hi%d" % m) for m in range(4)]
+        res = [keep.tile([P, S], F32, name="res%d" % m) for m in range(4)]
+
+        def b_window(m, engine):
+            evacuate(engine, b_win[m][:, :S], b_ps[m][:], 0.0625)
+
+        def low(m):
+            nc.vector.scalar_tensor_tensor(lo[m][:], b_ps[m][:], 0.0625, g5[m], ALU.mult, ALU.min)
+
+        def fetch_b(m, c0, c1):
+            nc.scalar.activation(g6[m][:, c0:c1], b_win[m][:].indirect(n6_t[:, c0 // 16 : c1 // 16]), COPY)
+
+        def finish(m, c0, c1, eng):
+            nc.vector.tensor_tensor(hi[m][:, c0:c1], a_ps[m][:, c0:c1], g6[m][:, c0:c1], ALU.max)
+            eng.tensor_tensor(res[m][:, c0:c1], hi[m][:, c0:c1], lo[m][:, c0:c1], ALU.subtract)
+            nc.sync.dma_start(out[P * m : P * (m + 1), c0:c1], res[m][:, c0:c1])
+
+        b_window(0, "vector")
+        low(0)
+        gather("vector", g6[0][:], b_win[0], n6_t)
         for m in range(1, 4):
-            if m >= 2:
-                nc.scalar.activation(s2_win[m][:, :S], b_ps[m][:], COPY, scale=0.0625)
-            gather("scalar", g6[m][:], s2_win[m], n6_t)
-        for m in range(4):
-            lo = keep.tile([P, S], F32, name="lo%d" % m)
-            nc.vector.scalar_tensor_tensor(lo[:], b_ps[m][:], 0.0625, g5[m][:], ALU.mult, ALU.min)
-            hi = keep.tile([P, S], F32, name="hi%d" % m)
-            nc.vector.tensor_tensor(hi[:], a_ps[m][:], g6[m][:], ALU.max)
-            res = keep.tile([P, S], F32, name="res%d" % m)
-            eng = nc.vector if m == 3 else nc.gpsimd
-            eng.tensor_tensor(res[:], hi[:], lo[:], ALU.subtract)
-            nc.sync.dma_start(out[P * m : P * (m + 1), :], res[:])
+            b_window(m, "scalar")
+        fetch_b(1, 0, S)
+        fetch_b(2, 0, S)
+        fetch_b(3, 0, S // 2)
+        fetch_b(3, S // 2, S)
+        for m in range(2):
+            low(m + 1)
+            finish(m, 0, S, nc.gpsimd)
+        low(3)
+        finish(2, 0, S, nc.vector)
+        finish(3, 0, S // 2, nc.vector)
+        finish(3, S // 2, S, nc.vector)

@@ -53,11 +53,8 @@ def tile_picked_fkcdmaxbhopbhopmx_none_p_kernel(
         xs = keep.tile([P, T], U8, name="xs", align_bytes=64)
         nc.vector.memset(xs[:].bitcast(I32), 0)
         for q in range(4):
-            nc.scalar.dma_start(xs[32 * q : 32 * q + 4, :].bitcast(I32), x_scales[0, 4 * q : 4 * q + 4, :].bitcast(I32))
+            nc.sync.dma_start(xs[32 * q : 32 * q + 4, :].bitcast(I32), x_scales[0, 4 * q : 4 * q + 4, :].bitcast(I32))
         offs_t = load_list("offs_t", offs)
-        cand_t = load_list("cand_t", cand)
-        n1_t = load_list("n1_t", n1)
-        n3_t = load_list("n3_t", n3)
         xw = keep.tile([P, T], I32, name="xw", align_bytes=64)
         nc.sync.dma_start(xw[:], x_words[0].rearrange("p n t -> p (n t)").bitcast(I32))
         w1_raw = []
@@ -65,10 +62,13 @@ def tile_picked_fkcdmaxbhopbhopmx_none_p_kernel(
             r = keep.tile([P, PACK, 256], F32, name="w1_raw%d" % h)
             nc.sync.dma_start(r[:], w1.rearrange("(p j) c -> p j c", j=PACK)[:, :, 256 * h : 256 * (h + 1)])
             w1_raw.append(r)
-        n2_t = load_list("n2_t", n2)
-        n4_t = load_list("n4_t", n4)
+        cand_t = load_list("cand_t", cand)
+        n1_t = load_list("n1_t", n1)
+        n3_t = load_list("n3_t", n3)
         w2_raw = keep.tile([P, PACK, 512], F32, name="w2_raw")
         nc.sync.dma_start(w2_raw[:], w2.rearrange("(p j) c -> p j c", j=PACK))
+        n2_t = load_list("n2_t", n2)
+        n4_t = load_list("n4_t", n4)
         gn_t = keep.tile([P, PACK], F32, name="gn_t")
         nc.sync.dma_start(gn_t[:], gn.rearrange("(p t) o -> p (t o)", t=PACK))
         gs_t = keep.tile([P, PACK], F32, name="gs_t")
@@ -142,18 +142,19 @@ def tile_picked_fkcdmaxbhopbhopmx_none_p_kernel(
                 nc.scalar.activation(dst, src, COPY, scale=scale)
 
         for t in range(4):
-            evacuate("scalar", y_win[t][:, :S], y_ps[t][:], 1.0)
+            evacuate("vector" if t == 2 else "scalar", y_win[t][:, :S], y_ps[t][:], 1.0)
         g2 = [keep.tile([P, S], F32, name="g2_%d" % t) for t in range(4)]
         g4 = [keep.tile([P, S], F32, name="g4_%d" % t) for t in range(4)]
         planes = keep.tile([P, 4, S], F32, name="planes")
 
-        for t in range(4):
-            gather("vector", st_win[t][:, S:], y_win[t], n1_t)
+        for t in range(5):
+            if t < 4:
+                gather("vector", st_win[t][:, S:], y_win[t], n1_t)
+            if t > 0:
+                nc.vector.tensor_tensor(st_win[t - 1][:, :S], y_ps[t - 1][:], st_win[t - 1][:, S:], ALU.max)
         for t in range(4):
             gather("scalar", s2_win[t][:, S:], y_win[t], n3_t)
             nc.gpsimd.tensor_tensor(s2_win[t][:, :S], y_win[t][:, :S], s2_win[t][:, S:], ALU.subtract)
-        for t in range(4):
-            nc.vector.tensor_tensor(st_win[t][:, :S], y_ps[t][:], st_win[t][:, S:], ALU.max)
         for t in range(4):
             gather("scalar", g2[t][:], st_win[t], n2_t)
         nc.vector.quantize_mx(out=w2_w[:].bitcast(FP8X4), scales=w2_s[:], in_=w2_g[:])

from contextlib import ExitStack

import concourse.mybir as mybir

K, T, S = 512, 2048, 512
P = 128
PACK = 4
FLOPS = 3 * 2 * 512 * 512 * 512

F32 = mybir.dt.float32
BF16 = mybir.dt.bfloat16
I32 = mybir.dt.int32
U32 = mybir.dt.uint32
U16 = mybir.dt.uint16
U8 = mybir.dt.uint8
FP8X4 = mybir.dt.float8_e4m3fn_x4
ALU = mybir.AluOpType
COPY = mybir.ActivationFunctionType.Copy


def tile_picked_fkcdmaxbhopbhopmx_none_p_kernel(
    tc, x_words, x_scales, w1, gn, w2, gs, offs, n1, n2, n3, n4, cand, n5, n6, out
):
    nc = tc.nc
    with ExitStack() as ctx:
        keep = ctx.enter_context(tc.tile_pool(name="keep", bufs=1))
        reuse = ctx.enter_context(tc.tile_pool(name="reuse", bufs=1))
        psum = ctx.enter_context(tc.psum_pool(name="psum", bufs=1))

        def load_list(name, src):
            t = keep.tile([P, S // 16], U16, name=name)
            nc.sync.dma_start(t[:], src)
            return t

        def gather(engine, dst, window, offsets):
            if engine == "vector":
                nc.vector.tensor_copy(dst, window[:].indirect(offsets[:]))
            else:
                nc.scalar.activation(dst, window[:].indirect(offsets[:]), COPY)

        def mx(acc, lw, ls, m, rw, rs, c0=0, c1=S):
            cols = slice(P * m, P * (m + 1))
            nc.tensor.matmul_mx(
                out=acc[:, c0:c1],
                lhsT=lw[:, cols].bitcast(FP8X4),
                lhsT_scale=ls[:, cols],
                rhs=rw[:, c0:c1].bitcast(FP8X4),
                rhs_scale=rs[:, c0:c1],
                start=True,
                stop=True,
            )

        xs = keep.tile([P, T], U8, name="xs", align_bytes=64)
        nc.vector.memset(xs[:].bitcast(I32), 0)
        for q in range(4):
            nc.sync.dma_start(xs[32 * q : 32 * q + 4, :].bitcast(I32), x_scales[0, 4 * q : 4 * q + 4, :].bitcast(I32))
        offs_t = load_list("offs_t", offs)
        xw = keep.tile([P, T], I32, name="xw", align_bytes=64)
        nc.sync.dma_start(xw[:], x_words[0].rearrange("p n t -> p (n t)").bitcast(I32))
        w1_raw = []
        for h in range(2):
            r = keep.tile([P, PACK, 256], F32, name="w1_raw%d" % h)
            nc.sync.dma_start(r[:], w1.rearrange("(p j) c -> p j c", j=PACK)[:, :, 256 * h : 256 * (h + 1)])
            w1_raw.append(r)
        cand_t = load_list("cand_t", cand)
        n1_t = load_list("n1_t", n1)
        n3_t = load_list("n3_t", n3)
        w2_raw = keep.tile([P, PACK, 512], F32, name="w2_raw")
        nc.sync.dma_start(w2_raw[:], w2.rearrange("(p j) c -> p j c", j=PACK))
        n2_t = load_list("n2_t", n2)
        n4_t = load_list("n4_t", n4)
        gn_t = keep.tile([P, PACK], F32, name="gn_t")
        nc.sync.dma_start(gn_t[:], gn.rearrange("(p t) o -> p (t o)", t=PACK))
        gs_t = keep.tile([P, PACK], F32, name="gs_t")
        nc.sync.dma_start(gs_t[:], gs.rearrange("(p t) o -> p (t o)", t=PACK))
        n5_t = load_list("n5_t", n5)
        n6_t = load_list("n6_t", n6)

        y_win = [keep.tile([P, 2 * S], F32, name="y_win%d" % t) for t in range(4)]
        st_win = [keep.tile([P, 2 * S], F32, name="st_win%d" % t) for t in range(4)]
        s2_win = [keep.tile([P, 2 * S], F32, name="s2_win%d" % t) for t in range(4)]
        for t in range(4):
            nc.vector.memset(y_win[t][:, S:], 0.0)

        def scale_quantise(name, planes, gain):
            grouped = keep.tile([P, 4 * S], BF16, name=name + "_g", align_bytes=64)
            words = keep.tile([P, S], U32, name=name + "_w", align_bytes=64)
            scales = keep.tile([P, S], U8, name=name + "_s", align_bytes=64)
            gv = grouped[:].rearrange("p (c i t) -> p c t i", i=4, t=4)
            pv = planes[:].rearrange("p t (c i) -> p c t i", i=4)
            gb = gain[:].unsqueeze(1).unsqueeze(3).to_broadcast([P, 64, 4, 4])
            for h in range(2):
                nc.vector.tensor_tensor(gv[:, 64 * h : 64 * (h + 1)], pv[:, 64 * h : 64 * (h + 1)], gb, ALU.mult)
            for h in range(2):
                cols = slice(256 * h, 256 * (h + 1))
                nc.vector.quantize_mx(
                    out=words[:, cols].bitcast(FP8X4), scales=scales[:, cols], in_=grouped[:, 1024 * h : 1024 * (h + 1)]
                )
            return words, scales

        pick_w = keep.tile([P, S], U32, name="pick_w", align_bytes=64)
        pick_s = keep.tile([P, S], U8, name="pick_s", align_bytes=64)
        nc.vector.tensor_copy(pick_w[:], xw[:].bitcast(U32).indirect(offs_t[:]))
        nc.vector.tensor_copy(pick_s[:], xs[:].indirect(offs_t[:]))

        w1_g = reuse.tile([P, 4 * 512], BF16, name="w1_g", offset=0, align_bytes=64)
        w1_v = w1_g[:].rearrange("p (t m j) -> p m j t", t=4, j=4)
        w1_r = [r[:].rearrange("p j (m t) -> p m j t", t=4) for r in w1_raw]
        nc.scalar.copy(w1_v[:, :64], w1_r[0])
        nc.scalar.copy(w1_v[:, 64:88], w1_r[1][:, :24])
        nc.vector.tensor_copy(w1_v[:, 88:], w1_r[1][:, 24:])
        w1_w = keep.tile([P, 512], U32, name="w1_w", align_bytes=64)
        w1_s = keep.tile([P, 512], U8, name="w1_s", align_bytes=64)
        y_ps = []
        for t in range(4):
            cols = slice(P * t, P * (t + 1))
            nc.vector.quantize_mx(out=w1_w[:, cols].bitcast(FP8X4), scales=w1_s[:, cols], in_=w1_g[:, 512 * t : 512 * (t + 1)])
            acc = psum.tile([P, S], F32, name="y_ps%d" % t, tag="yb%d" % t)
            mx(acc, w1_w, w1_s, t, pick_w, pick_s)
            y_ps.append(acc)
        cand_w = reuse.tile([P, S], U32, name="cand_w", offset=0, align_bytes=64)
        cand_s = reuse.tile([P, S], U8, name="cand_s", offset=2048, align_bytes=64)
        nc.vector.tensor_copy(cand_w[:], xw[:].bitcast(U32).indirect(cand_t[:]))
        nc.vector.tensor_copy(cand_s[:], xs[:].indirect(cand_t[:]))

        w2_g = keep.tile([P, 4 * 512], BF16, name="w2_g", align_bytes=64)
        nc.gpsimd.tensor_scalar(
            w2_g[:].rearrange("p (c j) -> p c j", j=4),
            w2_raw[:].rearrange("p j c -> p c j"),
            1.0,
            0.0,
            ALU.mult,
            ALU.add,
        )
        w2_w = keep.tile([P, 512], U32, name="w2_w", align_bytes=64)
        w2_s = keep.tile([P, 512], U8, name="w2_s", align_bytes=64)

        def evacuate(engine, dst, src, scale):
            if engine == "vector":
                nc.vector.tensor_scalar(dst, src, scale, None, ALU.mult)
            else:
                nc.scalar.activation(dst, src, COPY, scale=scale)

        for t in range(4):
            evacuate("vector" if t == 2 else "scalar", y_win[t][:, :S], y_ps[t][:], 1.0)
        g2 = [keep.tile([P, S], F32, name="g2_%d" % t) for t in range(4)]
        g4 = [keep.tile([P, S], F32, name="g4_%d" % t) for t in range(4)]
        planes = keep.tile([P, 4, S], F32, name="planes")

        for t in range(5):
            if t < 4:
                gather("vector", st_win[t][:, S:], y_win[t], n1_t)
            if t > 0:
                nc.vector.tensor_tensor(st_win[t - 1][:, :S], y_ps[t - 1][:], st_win[t - 1][:, S:], ALU.max)
        for t in range(4):
            gather("scalar", s2_win[t][:, S:], y_win[t], n3_t)
            nc.gpsimd.tensor_tensor(s2_win[t][:, :S], y_win[t][:, :S], s2_win[t][:, S:], ALU.subtract)
        for t in range(4):
            gather("scalar", g2[t][:], st_win[t], n2_t)
        nc.vector.quantize_mx(out=w2_w[:].bitcast(FP8X4), scales=w2_s[:], in_=w2_g[:])
        for t in range(4):
            nc.vector.scalar_tensor_tensor(planes[:, t, :], y_ps[t][:], -0.5, g2[t][:], ALU.mult, ALU.add)
        z_w, z_s = scale_quantise("z", planes, gn_t)
        a_ps = []
        for m in range(4):
            acc = psum.tile([P, S], F32, name="a_ps%d" % m, tag="ab%d" % m)
            mx(acc, w2_w, w2_s, m, z_w, z_s)
            a_ps.append(acc)

        for t in range(4):
            gather("scalar", g4[t][:], s2_win[t], n4_t)
        for t in range(4):
            nc.vector.tensor_tensor(planes[:, t, :], s2_win[t][:, :S], g4[t][:], ALU.max)
        z2_w, z2_s = scale_quantise("z2", planes, gs_t)

        a_win, b_win = st_win, s2_win
        g5 = [g2[0][:], g2[1][:], g2[2][:], planes[:, 3, :]]
        for m in range(4):
            evacuate("scalar", a_win[m][:, :S], a_ps[m][:], 1.0)
        for m in range(4):
            gather("vector" if m == 3 else "scalar", g5[m], a_win[m], n5_t)

        b_ps = []
        for m in range(4):
            acc = psum.tile([P, S], F32, name="b_ps%d" % m, tag="yb%d" % m)
            mx(acc, cand_w, cand_s, m, z2_w, z2_s, 0, S // 2)
            mx(acc, cand_w, cand_s, m, z2_w, z2_s, S // 2, S)
            b_ps.append(acc)
        g6 = g4
        lo = [keep.tile([P, S], F32, name="lo%d" % m) for m in range(4)]
        hi = [keep.tile([P, S], F32, name="hi%d" % m) for m in range(4)]
        res = [keep.tile([P, S], F32, name="res%d" % m) for m in range(4)]

        def b_window(m, engine):
            evacuate(engine, b_win[m][:, :S], b_ps[m][:], 0.0625)

        def low(m):
            nc.vector.scalar_tensor_tensor(lo[m][:], b_ps[m][:], 0.0625, g5[m], ALU.mult, ALU.min)

        def fetch_b(m, c0, c1):
            nc.scalar.activation(g6[m][:, c0:c1], b_win[m][:].indirect(n6_t[:, c0 // 16 : c1 // 16]), COPY)

        def finish(m, c0, c1, eng):
            nc.vector.tensor_tensor(hi[m][:, c0:c1], a_ps[m][:, c0:c1], g6[m][:, c0:c1], ALU.max)
            eng.tensor_tensor(res[m][:, c0:c1], hi[m][:, c0:c1], lo[m][:, c0:c1], ALU.subtract)
            nc.sync.dma_start(out[P * m : P * (m + 1), c0:c1], res[m][:, c0:c1])

        b_window(0, "vector")
        low(0)
        gather("vector", g6[0][:], b_win[0], n6_t)
        for m in range(1, 4):
            b_window(m, "scalar")
        fetch_b(1, 0, S)
        fetch_b(2, 0, S)
        fetch_b(3, 0, S // 2)
        fetch_b(3, S // 2, S)
        for m in range(2):
            low(m + 1)
            finish(m, 0, S, nc.gpsimd)
        low(3)
        finish(2, 0, S, nc.vector)
        finish(3, 0, S // 2, nc.vector)
        finish(3, S // 2, S, nc.vector)
